import numpy as np
import ml_dtypes


def mxq(x, axis, fmt="e4m3"):
    dtype, down = {"e4m3": (ml_dtypes.float8_e4m3fn, 7), "e5m2": (ml_dtypes.float8_e5m2, 14)}[fmt]
    v = np.moveaxis(np.asarray(x, np.float32).astype(ml_dtypes.bfloat16).astype(np.float64), axis, -1)
    blocks = v.reshape(v.shape[:-1] + (-1, 32))
    amax = np.abs(blocks).max(-1, keepdims=True)
    byte = np.maximum(np.where(amax > 0, np.frexp(amax)[1] - 1 + 127, 0) - down, 1)
    scale = np.exp2(byte - 127.0)
    codes = (blocks / scale).astype(np.float32).astype(dtype).astype(np.float64)
    return np.moveaxis((codes * scale).reshape(v.shape), -1, axis)


WIDE = False


def mx_kscale(k):
    if not WIDE:
        return np.ones(k)
    levels = np.array([10, -10, 5, -5, 0])
    if k % 512:
        return np.exp2(np.random.permutation(np.resize(levels, k // 32))).repeat(32)
    a = np.empty((k // 512, 16))
    for p in range(k // 512):
        a[p, :8] = np.random.permutation(np.resize(levels, 8))
        for g in range(8):
            far = levels[np.abs(levels - a[p, g]) >= 10]
            a[p, g + 8] = far[np.random.randint(len(far))]
    return np.exp2(a.ravel()).repeat(32)


def f64(x):
    return np.asarray(x).astype(np.float64)


def striped(idx):
    return np.tile(idx.reshape(-1, 16).T, (8, 1)).astype(np.uint16)


def unstriped(offs):
    return offs[:16].T.reshape(-1).astype(np.int64)


def striped8(idx):
    return np.concatenate([x.reshape(-1, 16).T for x in idx]).astype(np.uint16)


def runs(offs, k):
    lists = np.stack([offs[16 * r : 16 * r + 16].T.reshape(-1) for r in range(8)]).astype(np.int64)
    return lists[np.arange(k) % 512 // 64]


def pack_weight(w):
    k, n = w.shape
    w = f64(np.asarray(w, np.float32).astype(ml_dtypes.bfloat16)).reshape(k // 32, 32, n)
    amax = np.abs(w).max(1)
    byte = np.clip(np.where(amax > 0, np.frexp(amax)[1] - 1 + 127 - 7, 1), 1, 254)
    scaled = (w * np.exp2(127.0 - byte)[:, None, :]).reshape(k, n).astype(np.float32)
    words = np.ascontiguousarray(scaled.reshape(k // 512, 128, 4, n).transpose(0, 1, 3, 2)).astype(ml_dtypes.float8_e4m3fn).view(np.uint8)
    return words, np.ascontiguousarray(byte.astype(np.uint8).reshape(k // 512, 16, n))


def unpack_weight(words, scales):
    g, p, n, _ = words.shape
    vals = np.ascontiguousarray(words).view(ml_dtypes.float8_e4m3fn).astype(np.float64) * np.repeat(np.exp2(scales.astype(np.float64) - 127.0), 8, axis=1)[..., None]
    return vals.transpose(0, 1, 3, 2).reshape(g * 512, n)


K, T, S, G, H, W, U = 512, 1024, 256, 2048, 512, 128, 512


def setup_inputs():
    n = np.random.standard_normal
    s = mx_kscale(K)[:, None]
    packed_xT = pack_weight(n((K, T)) * s)
    packed_dT = pack_weight(n((K, G)) / s)
    perm = np.random.permutation(S)
    perm2 = np.random.permutation(U)
    return {
        "x_words": packed_xT[0],
        "x_scales": packed_xT[1],
        "d_words": packed_dT[0],
        "d_scales": packed_dT[1],
        "gs": (np.random.uniform(0.5, 1.5, (K, 1)) * s).astype(np.float32),
        "offs": striped(np.random.permutation(T)[:S]),
        "ci": striped(np.random.permutation(G)[:H]),
        "n1": striped(perm[:W]),
        "n2": striped(perm[W:]),
        "n3": striped(np.random.permutation(S)),
        "k1": striped8(np.random.randint(0, G, (8, H))),
        "k2": striped8(np.random.randint(0, G, (8, H))),
        "two": striped(np.random.permutation(T)[:S]),
        "n4": striped(perm2[:S]),
        "n5": striped(perm2[S:]),
        "n6": striped(np.random.permutation(S)),
        "n7": striped(np.random.permutation(S)),
    }


def reference(x_words, x_scales, d_words, d_scales, gs, offs, ci, n1, n2, n3, k1, k2, two, n4, n5, n6, n7):
    d_k1 = unpack_weight(d_words, d_scales)[np.arange(K)[:, None], runs(k1, K)]
    d_ci = unpack_weight(d_words, d_scales)[:, unstriped(ci)]
    xq = unpack_weight(x_words, x_scales)[:, unstriped(offs)]
    s = 0.0625 * (d_ci.T @ xq)
    pa = s[:, unstriped(n1)]
    pb = s[:, unstriped(n2)]
    rb = pa - pb
    ua = np.zeros((H, S))
    ua[:, unstriped(n1)] = pb
    ub = ua.copy()
    ub[:, unstriped(n2)] = rb
    z = f64(gs) * (np.maximum(ub, 0.5 * ub[:, unstriped(n3)]))
    d_k2 = unpack_weight(d_words, d_scales)[np.arange(K)[:, None], runs(k2, K)]
    x_two = unpack_weight(x_words, x_scales)[:, unstriped(two)]
    h2 = 0.0625 * ((d_k1.T @ mxq(z, 0, "e4m3") + d_k2.T @ x_two))
    st = h2 - h2[:, unstriped(n6)]
    up = np.maximum(st, st[:, unstriped(n7)])
    ph = np.zeros((H, U))
    ph[:, unstriped(n4)] = st
    out = ph.copy()
    out[:, unstriped(n5)] = up
    return out

@@ -1,0 +1,188 @@
+from contextlib import ExitStack
+
+import concourse.mybir as mybir
+
+F32 = mybir.dt.float32
+BF16 = mybir.dt.bfloat16
+I32 = mybir.dt.int32
+U32 = mybir.dt.uint32
+U16 = mybir.dt.uint16
+U8 = mybir.dt.uint8
+FP8X4 = mybir.dt.float8_e4m3fn_x4
+ALU = mybir.AluOpType
+COPY = mybir.ActivationFunctionType.Copy
+
+P = 128
+T, S, G, H, W, U = 1024, 256, 2048, 512, 128, 512
+NT = 4
+HALF = S // 2
+FLOPS = 3 * 2 * 512 * H * S
+
+
+def tile_picked_xtzmtswapdpagew_none_p_kernel(
+    tc, x_words, x_scales, d_words, d_scales, gs, offs, ci, n1, n2, n3, k1, k2, two, n4, n5, n6, n7, out
+):
+    nc = tc.nc
+    with ExitStack() as ctx:
+        lists = ctx.enter_context(tc.tile_pool(name="lists", bufs=1))
+        keep = ctx.enter_context(tc.tile_pool(name="keep", bufs=1))
+        psum = ctx.enter_context(tc.psum_pool(name="psum", bufs=1))
+
+        def load_list(name, src):
+            held = lists.tile(list(src.shape), U16, name=name)
+            nc.sync.dma_start(out=held[:], in_=src)
+            return held
+
+        dw = keep.tile([P, G], U32, name="dw", align_bytes=64)
+        xw = keep.tile([P, T], U32, name="xw", align_bytes=64)
+        ds = keep.tile([P, G], U8, name="ds", align_bytes=64)
+        xs = keep.tile([P, T], U8, name="xs", align_bytes=64)
+        gs_t = keep.tile([P, NT], F32, name="gs_t")
+        d_rows = d_scales[0].bitcast(I32)
+        x_rows = x_scales[0].bitcast(I32)
+
+        nc.vector.memset(ds[:].bitcast(I32), 0)
+        nc.gpsimd.memset(xs[:].bitcast(I32), 0)
+        offs_l = load_list("offs_l", offs)
+        ci_l = load_list("ci_l", ci)
+        nc.sync.dma_start(out=xw[:].bitcast(I32), in_=x_words[0].rearrange("p n t -> p (n t)").bitcast(I32))
+        for r in range(2):
+            nc.sync.dma_start(out=ds[r:P:16, :].bitcast(I32), in_=d_rows[r:16:2, :])
+        for r in range(2, 4):
+            nc.sync.dma_start(out=ds[r:P:32, :].bitcast(I32), in_=d_rows[r:16:4, :])
+        nc.sync.dma_start(out=dw[:].bitcast(I32), in_=d_words[0].rearrange("p n t -> p (n t)").bitcast(I32))
+        for q in range(4):
+            queue = nc.sync if q < 2 else nc.gpsimd
+            queue.dma_start(out=xs[32 * q : 32 * q + 4, :].bitcast(I32), in_=x_rows[4 * q : 4 * q + 4, :])
+        nc.gpsimd.dma_start(out=gs_t[:], in_=gs.rearrange("(p t) o -> p (t o)", t=NT))
+        n1_l = load_list("n1_l", n1)
+        n2_l = load_list("n2_l", n2)
+        n3_l = load_list("n3_l", n3)
+        k1_l = load_list("k1_l", k1)
+        k2_l = load_list("k2_l", k2)
+        two_l = load_list("two_l", two)
+        n6_l = load_list("n6_l", n6)
+        n7_l = load_list("n7_l", n7)
+        n4_l = load_list("n4_l", n4)
+        n5_l = load_list("n5_l", n5)
+
+        def gather_v(dst, window, offsets):
+            nc.vector.tensor_copy(out=dst, in_=window[:].indirect(offsets[:]))
+
+        def gather_s(dst, window, offsets):
+            nc.scalar.activation(out=dst, in_=window.indirect(offsets), func=COPY)
+
+        def scatter_s(window, offsets, src):
+            nc.scalar.activation(out=window[:].indirect(offsets[:]), in_=src, func=COPY)
+
+        ci_b = keep.tile([P, H], U8, name="ci_b", tag="pick_db", align_bytes=64)
+        offs_b = keep.tile([P, S], U8, name="offs_b", tag="pick_xb", align_bytes=64)
+        ci_w = keep.tile([P, H], U32, name="ci_w", tag="pick_dw", align_bytes=64)
+        offs_w = keep.tile([P, S], U32, name="offs_w", tag="pick_xw", align_bytes=64)
+        gather_v(offs_w[:], xw, offs_l)
+        gather_v(ci_b[:].rearrange("p (t m) -> p m t", t=NT), ds, ci_l)
+        gather_v(offs_b[:], xs, offs_l)
+        gather_v(ci_w[:].rearrange("p (t m) -> p m t", t=NT), dw, ci_l)
+
+        ub_s = [keep.tile([P, 2 * S], F32, name=f"ub_s{t}") for t in range(NT)]
+        for t in range(NT):
+            cols = slice(t * P, (t + 1) * P)
+            acc = psum.tile([P, S], F32, name=f"s_acc{t}", tag=f"bank{t}")
+            nc.tensor.matmul_mx(
+                out=acc[:], lhsT=ci_w[:, cols].bitcast(FP8X4), lhsT_scale=ci_b[:, cols],
+                rhs=offs_w[:].bitcast(FP8X4), rhs_scale=offs_b[:], start=True, stop=True,
+            )
+            if t == 0:
+                nc.scalar.activation(out=ub_s[t][:, S:], in_=acc[:], func=COPY, scale=0.0625)
+            else:
+                nc.vector.tensor_scalar(out=ub_s[t][:, S:], in0=acc[:], scalar1=0.0625, scalar2=None, op0=ALU.mult)
+
+        pa = [keep.tile([P, W], F32, name=f"pa{t}") for t in range(NT)]
+        pb = [keep.tile([P, W], F32, name=f"pb{t}") for t in range(NT)]
+        rb = [keep.tile([P, W], F32, name=f"rb{t}") for t in range(NT)]
+        for t in range(NT):
+            gather_s(pa[t][:], ub_s[t][:, S:], n1_l[:])
+            gather_s(pb[t][:], ub_s[t][:, S:], n2_l[:])
+            nc.vector.tensor_tensor(out=rb[t][:], in0=pa[t][:], in1=pb[t][:], op=ALU.subtract)
+        for t in range(NT):
+            scatter_s(ub_s[t], n1_l, pb[t][:])
+
+        k_b = keep.tile([P, 2 * H], U8, name="k_b", tag="pick_db", align_bytes=64)
+        gather_v(k_b[:, :H], ds, k1_l)
+        gather_v(k_b[:, H:], ds, k2_l)
+        k_plane = keep.tile([P, 2 * H], U8, name="k_plane", align_bytes=64)
+        nc.vector.tensor_copy(out=k_plane[:].bitcast(I32), in_=k_b[:].bitcast(I32))
+        for r in range(2):
+            nc.sync.dma_start(out=k_plane[2 + r : P : 32, :].bitcast(I32), in_=k_b[16 + r : P : 32, :].bitcast(I32))
+        two_b = keep.tile([P, S], U8, name="two_b", tag="pick_xb", align_bytes=64)
+        gather_v(two_b[:], xs, two_l)
+        k_w = keep.tile([P, 2 * H], U32, name="k_w", tag="pick_dw", align_bytes=64)
+        two_w = keep.tile([P, S], U32, name="two_w", tag="pick_xw", align_bytes=64)
+        gather_v(two_w[:], xw, two_l)
+        gather_v(k_w[:, H:], dw, k2_l)
+        gather_v(k_w[:, :H], dw, k1_l)
+
+        h2_m = [keep.tile([P, 2 * S], F32, name=f"h2_m{t}") for t in range(NT)]
+        ub3 = [keep.tile([P, S], F32, name=f"ub3_{t}") for t in range(NT)]
+        z_bf = keep.tile([P, S, NT], BF16, name="z_bf", align_bytes=64)
+        z_w = keep.tile([P, S], U32, name="z_w", align_bytes=64)
+        z_b = keep.tile([P, S], U8, name="z_b", align_bytes=64)
+        halves = [slice(0, HALF), slice(HALF, S)]
+        for t in range(NT):
+            scatter_s(ub_s[t], n2_l, rb[t][:])
+            for cols in halves if t == NT - 1 else [slice(0, S)]:
+                gather_s(ub3[t][:, cols], ub_s[t][:], n3_l[:, cols.start // 16 : cols.stop // 16])
+                larger = h2_m[t][:, S + cols.start : S + cols.stop]
+                nc.vector.scalar_tensor_tensor(
+                    out=larger, in0=ub3[t][:, cols], scalar=0.5, in1=ub_s[t][:, cols], op0=ALU.mult, op1=ALU.max
+                )
+                nc.vector.tensor_scalar(
+                    out=z_bf[:, cols, t], in0=larger, scalar1=gs_t[:, t : t + 1], scalar2=None, op0=ALU.mult
+                )
+                if t == NT - 1:
+                    nc.vector.quantize_mx(
+                        out=z_w[:, cols].bitcast(FP8X4), scales=z_b[:, cols],
+                        in_=z_bf[:, cols, :].rearrange("p c t -> p (c t)"),
+                    )
+
+        groups = [(0, halves[0]), (0, halves[1])] + [(t, slice(0, S)) for t in range(1, NT)]
+        accs = [
+            psum.tile([P, cols.stop - cols.start], F32, name=f"h_acc{g}", tag=f"bank{(4 + g) % 8}")
+            for g, (t, cols) in enumerate(groups)
+        ]
+        for acc, (t, cols) in zip(accs, groups):
+            rows = slice(H + t * P, H + (t + 1) * P)
+            nc.tensor.matmul_mx(
+                out=acc[:], lhsT=k_w[:, rows].bitcast(FP8X4), lhsT_scale=k_plane[:, rows],
+                rhs=two_w[:, cols].bitcast(FP8X4), rhs_scale=two_b[:, cols], start=True, stop=False,
+            )
+        for g, (acc, (t, cols)) in enumerate(zip(accs, groups)):
+            rows = slice(t * P, (t + 1) * P)
+            nc.tensor.matmul_mx(
+                out=acc[:], lhsT=k_w[:, rows].bitcast(FP8X4), lhsT_scale=k_plane[:, rows],
+                rhs=z_w[:, cols].bitcast(FP8X4), rhs_scale=z_b[:, cols], start=False, stop=True,
+            )
+            if t == 0:
+                nc.scalar.activation(out=h2_m[t][:, cols], in_=acc[:], func=COPY, scale=0.0625)
+            else:
+                nc.vector.tensor_scalar(out=h2_m[t][:, cols], in0=acc[:], scalar1=0.0625, scalar2=None, op0=ALU.mult)
+
+        st_g = [keep.tile([P, 2 * S], F32, name=f"st_g{t}") for t in range(NT)]
+        st7 = [keep.tile([P, S], F32, name=f"st7_{t}") for t in range(NT)]
+        up = [keep.tile([P, S], F32, name=f"up{t}") for t in range(NT)]
+        page = [keep.tile([P, U], F32, name=f"page{t}") for t in range(NT)]
+
+        def make_st(t):
+            gather_s(st_g[t][:, S:], h2_m[t][:], n6_l[:])
+            nc.vector.tensor_tensor(out=st_g[t][:, :S], in0=h2_m[t][:, :S], in1=st_g[t][:, S:], op=ALU.subtract)
+
+        make_st(0)
+        make_st(1)
+        for t in range(NT):
+            gather_s(st7[t][:], st_g[t][:], n7_l[:])
+            nc.vector.tensor_tensor(out=up[t][:], in0=st_g[t][:, :S], in1=st7[t][:], op=ALU.max)
+            scatter_s(page[t], n4_l, st_g[t][:, :S])
+            if t + 2 < NT:
+                make_st(t + 2)
+            scatter_s(page[t], n5_l, up[t][:])
+            nc.sync.dma_start(out=out[t * P : (t + 1) * P, :], in_=page[t][:])

@@ -128,22 +128,45 @@ def tile_picked_xtzmtswapdpagew_none_p_kernel(
         z_w = keep.tile([P, S], U32, name="z_w", align_bytes=64)
         z_b = keep.tile([P, S], U8, name="z_b", align_bytes=64)
         halves = [slice(0, HALF), slice(HALF, S)]
-        for t in range(NT):
+
+        def larger(t, cols):
+            return h2_m[t][:, S + cols.start : S + cols.stop]
+
+        def take_larger(t, cols):
+            gather_s(ub3[t][:, cols], ub_s[t][:], n3_l[:, cols.start // 16 : cols.stop // 16])
+            nc.vector.scalar_tensor_tensor(
+                out=larger(t, cols), in0=ub3[t][:, cols], scalar=0.5, in1=ub_s[t][:, cols], op0=ALU.mult, op1=ALU.max
+            )
+
+        def weigh(t, cols):
+            nc.vector.tensor_scalar(
+                out=z_bf[:, cols, t], in0=larger(t, cols), scalar1=gs_t[:, t : t + 1], scalar2=None, op0=ALU.mult
+            )
+
+        def quantise(cols):
+            nc.vector.quantize_mx(
+                out=z_w[:, cols].bitcast(FP8X4), scales=z_b[:, cols],
+                in_=z_bf[:, cols, :].rearrange("p c t -> p (c t)"),
+            )
+
+        left, right = halves
+        last = NT - 1
+        scatter_s(ub_s[0], n2_l, rb[0][:])
+        for t in range(1, last):
             scatter_s(ub_s[t], n2_l, rb[t][:])
-            for cols in halves if t == NT - 1 else [slice(0, S)]:
-                gather_s(ub3[t][:, cols], ub_s[t][:], n3_l[:, cols.start // 16 : cols.stop // 16])
-                larger = h2_m[t][:, S + cols.start : S + cols.stop]
-                nc.vector.scalar_tensor_tensor(
-                    out=larger, in0=ub3[t][:, cols], scalar=0.5, in1=ub_s[t][:, cols], op0=ALU.mult, op1=ALU.max
-                )
-                nc.vector.tensor_scalar(
-                    out=z_bf[:, cols, t], in0=larger, scalar1=gs_t[:, t : t + 1], scalar2=None, op0=ALU.mult
-                )
-                if t == NT - 1:
-                    nc.vector.quantize_mx(
-                        out=z_w[:, cols].bitcast(FP8X4), scales=z_b[:, cols],
-                        in_=z_bf[:, cols, :].rearrange("p c t -> p (c t)"),
-                    )
+            take_larger(t - 1, slice(0, S))
+            weigh(t - 1, slice(0, S))
+        take_larger(last - 1, left)
+        weigh(last - 1, left)
+        scatter_s(ub_s[last], n2_l, rb[last][:])
+        take_larger(last - 1, right)
+        weigh(last - 1, right)
+        for cols in halves:
+            take_larger(last, cols)
+        for cols in halves:
+            weigh(last, cols)
+        for cols in halves:
+            quantise(cols)
 
         groups = [(0, halves[0]), (0, halves[1])] + [(t, slice(0, S)) for t in range(1, NT)]
         accs = [
@@ -176,13 +199,20 @@ def tile_picked_xtzmtswapdpagew_none_p_kernel(
             gather_s(st_g[t][:, S:], h2_m[t][:], n6_l[:])
             nc.vector.tensor_tensor(out=st_g[t][:, :S], in0=h2_m[t][:, :S], in1=st_g[t][:, S:], op=ALU.subtract)
 
-        make_st(0)
-        make_st(1)
-        for t in range(NT):
+        def make_up(t):
             gather_s(st7[t][:], st_g[t][:], n7_l[:])
             nc.vector.tensor_tensor(out=up[t][:], in0=st_g[t][:, :S], in1=st7[t][:], op=ALU.max)
-            scatter_s(page[t], n4_l, st_g[t][:, :S])
-            if t + 2 < NT:
-                make_st(t + 2)
+
+        def finish(t):
             scatter_s(page[t], n5_l, up[t][:])
             nc.sync.dma_start(out=out[t * P : (t + 1) * P, :], in_=page[t][:])
+
+        for t in range(NT):
+            make_st(t)
+        for t in range(NT):
+            make_up(t)
+        scatter_s(page[0], n4_l, st_g[0][:, :S])
+        for t in range(1, NT):
+            scatter_s(page[t], n4_l, st_g[t][:, :S])
+            finish(t - 1)
+        finish(NT - 1)

from contextlib import ExitStack

import concourse.mybir as mybir

F32 = mybir.dt.float32
BF16 = mybir.dt.bfloat16
I32 = mybir.dt.int32
U32 = mybir.dt.uint32
U16 = mybir.dt.uint16
U8 = mybir.dt.uint8
FP8X4 = mybir.dt.float8_e4m3fn_x4
ALU = mybir.AluOpType
COPY = mybir.ActivationFunctionType.Copy

P = 128
T, S, G, H, W, U = 1024, 256, 2048, 512, 128, 512
NT = 4
HALF = S // 2
FLOPS = 3 * 2 * 512 * H * S


def tile_picked_xtzmtswapdpagew_none_p_kernel(
    tc, x_words, x_scales, d_words, d_scales, gs, offs, ci, n1, n2, n3, k1, k2, two, n4, n5, n6, n7, out
):
    nc = tc.nc
    with ExitStack() as ctx:
        lists = ctx.enter_context(tc.tile_pool(name="lists", bufs=1))
        keep = ctx.enter_context(tc.tile_pool(name="keep", bufs=1))
        psum = ctx.enter_context(tc.psum_pool(name="psum", bufs=1))

        def load_list(name, src):
            held = lists.tile(list(src.shape), U16, name=name)
            nc.sync.dma_start(out=held[:], in_=src)
            return held

        dw = keep.tile([P, G], U32, name="dw", align_bytes=64)
        xw = keep.tile([P, T], U32, name="xw", align_bytes=64)
        ds = keep.tile([P, G], U8, name="ds", align_bytes=64)
        xs = keep.tile([P, T], U8, name="xs", align_bytes=64)
        gs_t = keep.tile([P, NT], F32, name="gs_t")
        d_rows = d_scales[0].bitcast(I32)
        x_rows = x_scales[0].bitcast(I32)

        nc.vector.memset(ds[:].bitcast(I32), 0)
        nc.gpsimd.memset(xs[:].bitcast(I32), 0)
        offs_l = load_list("offs_l", offs)
        ci_l = load_list("ci_l", ci)
        nc.sync.dma_start(out=xw[:].bitcast(I32), in_=x_words[0].rearrange("p n t -> p (n t)").bitcast(I32))
        for r in range(2):
            nc.sync.dma_start(out=ds[r:P:16, :].bitcast(I32), in_=d_rows[r:16:2, :])
        for r in range(2, 4):
            nc.sync.dma_start(out=ds[r:P:32, :].bitcast(I32), in_=d_rows[r:16:4, :])
        nc.sync.dma_start(out=dw[:].bitcast(I32), in_=d_words[0].rearrange("p n t -> p (n t)").bitcast(I32))
        for q in range(4):
            queue = nc.sync if q < 2 else nc.gpsimd
            queue.dma_start(out=xs[32 * q : 32 * q + 4, :].bitcast(I32), in_=x_rows[4 * q : 4 * q + 4, :])
        nc.gpsimd.dma_start(out=gs_t[:], in_=gs.rearrange("(p t) o -> p (t o)", t=NT))
        n1_l = load_list("n1_l", n1)
        n2_l = load_list("n2_l", n2)
        n3_l = load_list("n3_l", n3)
        k1_l = load_list("k1_l", k1)
        k2_l = load_list("k2_l", k2)
        two_l = load_list("two_l", two)
        n6_l = load_list("n6_l", n6)
        n7_l = load_list("n7_l", n7)
        n4_l = load_list("n4_l", n4)
        n5_l = load_list("n5_l", n5)

        def gather_v(dst, window, offsets):
            nc.vector.tensor_copy(out=dst, in_=window[:].indirect(offsets[:]))

        def gather_s(dst, window, offsets):
            nc.scalar.activation(out=dst, in_=window.indirect(offsets), func=COPY)

        def scatter_s(window, offsets, src):
            nc.scalar.activation(out=window[:].indirect(offsets[:]), in_=src, func=COPY)

        ci_b = keep.tile([P, H], U8, name="ci_b", tag="pick_db", align_bytes=64)
        offs_b = keep.tile([P, S], U8, name="offs_b", tag="pick_xb", align_bytes=64)
        ci_w = keep.tile([P, H], U32, name="ci_w", tag="pick_dw", align_bytes=64)
        offs_w = keep.tile([P, S], U32, name="offs_w", tag="pick_xw", align_bytes=64)
        gather_v(offs_w[:], xw, offs_l)
        gather_v(ci_b[:].rearrange("p (t m) -> p m t", t=NT), ds, ci_l)
        gather_v(offs_b[:], xs, offs_l)
        gather_v(ci_w[:].rearrange("p (t m) -> p m t", t=NT), dw, ci_l)

        ub_s = [keep.tile([P, 2 * S], F32, name=f"ub_s{t}") for t in range(NT)]
        for t in range(NT):
            cols = slice(t * P, (t + 1) * P)
            acc = psum.tile([P, S], F32, name=f"s_acc{t}", tag=f"bank{t}")
            nc.tensor.matmul_mx(
                out=acc[:], lhsT=ci_w[:, cols].bitcast(FP8X4), lhsT_scale=ci_b[:, cols],
                rhs=offs_w[:].bitcast(FP8X4), rhs_scale=offs_b[:], start=True, stop=True,
            )
            if t == 0:
                nc.scalar.activation(out=ub_s[t][:, S:], in_=acc[:], func=COPY, scale=0.0625)
            else:
                nc.vector.tensor_scalar(out=ub_s[t][:, S:], in0=acc[:], scalar1=0.0625, scalar2=None, op0=ALU.mult)

        pa = [keep.tile([P, W], F32, name=f"pa{t}") for t in range(NT)]
        pb = [keep.tile([P, W], F32, name=f"pb{t}") for t in range(NT)]
        rb = [keep.tile([P, W], F32, name=f"rb{t}") for t in range(NT)]
        for t in range(NT):
            gather_s(pa[t][:], ub_s[t][:, S:], n1_l[:])
            gather_s(pb[t][:], ub_s[t][:, S:], n2_l[:])
            nc.vector.tensor_tensor(out=rb[t][:], in0=pa[t][:], in1=pb[t][:], op=ALU.subtract)
        for t in range(NT):
            scatter_s(ub_s[t], n1_l, pb[t][:])

        k_b = keep.tile([P, 2 * H], U8, name="k_b", tag="pick_db", align_bytes=64)
        gather_v(k_b[:, :H], ds, k1_l)
        gather_v(k_b[:, H:], ds, k2_l)
        k_plane = keep.tile([P, 2 * H], U8, name="k_plane", align_bytes=64)
        nc.vector.tensor_copy(out=k_plane[:].bitcast(I32), in_=k_b[:].bitcast(I32))
        for r in range(2):
            nc.sync.dma_start(out=k_plane[2 + r : P : 32, :].bitcast(I32), in_=k_b[16 + r : P : 32, :].bitcast(I32))
        two_b = keep.tile([P, S], U8, name="two_b", tag="pick_xb", align_bytes=64)
        gather_v(two_b[:], xs, two_l)
        k_w = keep.tile([P, 2 * H], U32, name="k_w", tag="pick_dw", align_bytes=64)
        two_w = keep.tile([P, S], U32, name="two_w", tag="pick_xw", align_bytes=64)
        gather_v(two_w[:], xw, two_l)
        gather_v(k_w[:, H:], dw, k2_l)
        gather_v(k_w[:, :H], dw, k1_l)

        h2_m = [keep.tile([P, 2 * S], F32, name=f"h2_m{t}") for t in range(NT)]
        ub3 = [keep.tile([P, S], F32, name=f"ub3_{t}") for t in range(NT)]
        z_bf = keep.tile([P, S, NT], BF16, name="z_bf", align_bytes=64)
        z_w = keep.tile([P, S], U32, name="z_w", align_bytes=64)
        z_b = keep.tile([P, S], U8, name="z_b", align_bytes=64)
        halves = [slice(0, HALF), slice(HALF, S)]

        def larger(t, cols):
            return h2_m[t][:, S + cols.start : S + cols.stop]

        def take_larger(t, cols):
            gather_s(ub3[t][:, cols], ub_s[t][:], n3_l[:, cols.start // 16 : cols.stop // 16])
            nc.vector.scalar_tensor_tensor(
                out=larger(t, cols), in0=ub3[t][:, cols], scalar=0.5, in1=ub_s[t][:, cols], op0=ALU.mult, op1=ALU.max
            )

        def weigh(t, cols):
            nc.vector.tensor_scalar(
                out=z_bf[:, cols, t], in0=larger(t, cols), scalar1=gs_t[:, t : t + 1], scalar2=None, op0=ALU.mult
            )

        def quantise(cols):
            nc.vector.quantize_mx(
                out=z_w[:, cols].bitcast(FP8X4), scales=z_b[:, cols],
                in_=z_bf[:, cols, :].rearrange("p c t -> p (c t)"),
            )

        left, right = halves
        last = NT - 1
        scatter_s(ub_s[0], n2_l, rb[0][:])
        for t in range(1, last):
            scatter_s(ub_s[t], n2_l, rb[t][:])
            take_larger(t - 1, slice(0, S))
            weigh(t - 1, slice(0, S))
        take_larger(last - 1, left)
        weigh(last - 1, left)
        scatter_s(ub_s[last], n2_l, rb[last][:])
        take_larger(last - 1, right)
        weigh(last - 1, right)
        for cols in halves:
            take_larger(last, cols)
        for cols in halves:
            weigh(last, cols)
        for cols in halves:
            quantise(cols)

        groups = [(0, halves[0]), (0, halves[1])] + [(t, slice(0, S)) for t in range(1, NT)]
        accs = [
            psum.tile([P, cols.stop - cols.start], F32, name=f"h_acc{g}", tag=f"bank{(4 + g) % 8}")
            for g, (t, cols) in enumerate(groups)
        ]
        for acc, (t, cols) in zip(accs, groups):
            rows = slice(H + t * P, H + (t + 1) * P)
            nc.tensor.matmul_mx(
                out=acc[:], lhsT=k_w[:, rows].bitcast(FP8X4), lhsT_scale=k_plane[:, rows],
                rhs=two_w[:, cols].bitcast(FP8X4), rhs_scale=two_b[:, cols], start=True, stop=False,
            )
        for g, (acc, (t, cols)) in enumerate(zip(accs, groups)):
            rows = slice(t * P, (t + 1) * P)
            nc.tensor.matmul_mx(
                out=acc[:], lhsT=k_w[:, rows].bitcast(FP8X4), lhsT_scale=k_plane[:, rows],
                rhs=z_w[:, cols].bitcast(FP8X4), rhs_scale=z_b[:, cols], start=False, stop=True,
            )
            if t == 0:
                nc.scalar.activation(out=h2_m[t][:, cols], in_=acc[:], func=COPY, scale=0.0625)
            else:
                nc.vector.tensor_scalar(out=h2_m[t][:, cols], in0=acc[:], scalar1=0.0625, scalar2=None, op0=ALU.mult)

        st_g = [keep.tile([P, 2 * S], F32, name=f"st_g{t}") for t in range(NT)]
        st7 = [keep.tile([P, S], F32, name=f"st7_{t}") for t in range(NT)]
        up = [keep.tile([P, S], F32, name=f"up{t}") for t in range(NT)]
        page = [keep.tile([P, U], F32, name=f"page{t}") for t in range(NT)]

        def make_st(t):
            gather_s(st_g[t][:, S:], h2_m[t][:], n6_l[:])
            nc.vector.tensor_tensor(out=st_g[t][:, :S], in0=h2_m[t][:, :S], in1=st_g[t][:, S:], op=ALU.subtract)

        def make_up(t):
            gather_s(st7[t][:], st_g[t][:], n7_l[:])
            nc.vector.tensor_tensor(out=up[t][:], in0=st_g[t][:, :S], in1=st7[t][:], op=ALU.max)

        def finish(t):
            scatter_s(page[t], n5_l, up[t][:])
            nc.sync.dma_start(out=out[t * P : (t + 1) * P, :], in_=page[t][:])

        for t in range(NT):
            make_st(t)
        for t in range(NT):
            make_up(t)
        scatter_s(page[0], n4_l, st_g[0][:, :S])
        for t in range(1, NT):
            scatter_s(page[t], n4_l, st_g[t][:, :S])
            finish(t - 1)
        finish(NT - 1)
